import numpy as np
import ml_dtypes


def mxq(x, axis, fmt="e4m3"):
    dtype, down = {"e4m3": (ml_dtypes.float8_e4m3fn, 7), "e5m2": (ml_dtypes.float8_e5m2, 14)}[fmt]
    v = np.moveaxis(np.asarray(x, np.float32).astype(ml_dtypes.bfloat16).astype(np.float64), axis, -1)
    blocks = v.reshape(v.shape[:-1] + (-1, 32))
    amax = np.abs(blocks).max(-1, keepdims=True)
    byte = np.maximum(np.where(amax > 0, np.frexp(amax)[1] - 1 + 127, 0) - down, 1)
    scale = np.exp2(byte - 127.0)
    codes = (blocks / scale).astype(np.float32).astype(dtype).astype(np.float64)
    return np.moveaxis((codes * scale).reshape(v.shape), -1, axis)


WIDE = False


def mx_kscale(k):
    if not WIDE:
        return np.ones(k)
    levels = np.array([10, -10, 5, -5, 0])
    if k % 512:
        return np.exp2(np.random.permutation(np.resize(levels, k // 32))).repeat(32)
    a = np.empty((k // 512, 16))
    for p in range(k // 512):
        a[p, :8] = np.random.permutation(np.resize(levels, 8))
        for g in range(8):
            far = levels[np.abs(levels - a[p, g]) >= 10]
            a[p, g + 8] = far[np.random.randint(len(far))]
    return np.exp2(a.ravel()).repeat(32)


def f64(x):
    return np.asarray(x).astype(np.float64)


def striped(idx):
    return np.tile(idx.reshape(-1, 16).T, (8, 1)).astype(np.uint16)


def unstriped(offs):
    return offs[:16].T.reshape(-1).astype(np.int64)


E2M1 = np.array([0.0, 0.5, 1.0, 1.5, 2.0, 3.0, 4.0, 6.0, -0.0, -0.5, -1.0, -1.5, -2.0, -3.0, -4.0, -6.0])


def pack_weight(w, fmt):
    k, n = w.shape
    w = f64(np.asarray(w, np.float32).astype(ml_dtypes.bfloat16)).reshape(k // 32, 32, n)
    amax = np.abs(w).max(1)
    if fmt == "e4m3":
        byte = np.frexp(amax)[1] - 1 + 127 - 7
    else:
        mant, ex = np.frexp(amax / 6.0)
        byte = np.where(mant > 0.5, ex, ex - 1) + 127
    byte = np.clip(np.where(amax > 0, byte, 1), 1, 254)
    scaled = (w * np.exp2(127.0 - byte)[:, None, :]).reshape(k, n).astype(np.float32)
    by_word = np.ascontiguousarray(scaled.reshape(k // 512, 128, 4, n).transpose(0, 1, 3, 2))
    if fmt == "e4m3":
        words = by_word.astype(ml_dtypes.float8_e4m3fn).view(np.uint8)
    else:
        c = by_word.astype(ml_dtypes.float4_e2m1fn).view(np.uint8) & 0xF
        words = (c[..., 0::2] | (c[..., 1::2] << 4)).reshape(k // 512, 128, 2 * n)
    return np.ascontiguousarray(words), np.ascontiguousarray(byte.astype(np.uint8).reshape(k // 512, 16, n))


def unpack_weight(words, scales, fmt):
    g, _, n = scales.shape
    words = np.ascontiguousarray(words).reshape(g, 128, n, -1)
    if fmt == "e4m3":
        vals = words.view(ml_dtypes.float8_e4m3fn).astype(np.float64)
    else:
        nib = np.empty((g, 128, n, 4), np.uint8)
        nib[..., 0::2] = words & 0xF
        nib[..., 1::2] = words >> 4
        vals = E2M1[nib]
    vals = vals * np.repeat(np.exp2(scales.astype(np.float64) - 127.0), 8, axis=1)[..., None]
    return vals.transpose(0, 1, 3, 2).reshape(g * 512, n)


def gelu(v):
    return 0.5 * v * (1.0 + np.tanh(np.sqrt(2.0 / np.pi) * (v + 0.044715 * v**3)))


def striped8(idx):
    return np.concatenate([v.reshape(-1, 16).T for v in idx]).astype(np.uint16)


def unstriped8(offs):
    return np.stack([offs[16 * g:16 * g + 16].T.reshape(-1) for g in range(8)]).astype(np.int64)


def heads(h, wgt, idx8):
    r = np.arange(h.shape[0])
    return wgt[r // 4 % 128] * h[r[:, None], idx8[r % 512 // 64]]


def put_heads(h, wgs, idx8, t2):
    r = np.arange(h.shape[0])
    page = np.zeros((h.shape[0], t2))
    page[r[:, None], idx8[r % 512 // 64]] = wgs[r // 4 % 128] * h
    return page


K, H, N, T, S, P, T2 = 1024, 1024, 512, 4096, 1024, 1024, 2048

def setup_inputs():
    n = np.random.standard_normal
    s = mx_kscale(K)[:, None]
    u = mx_kscale(H)[:, None]
    d = {}
    d["tab_words"], d["tab_scales"] = pack_weight(n((K, T)) * s, "e4m3")
    d["offs"] = striped(np.random.permutation(T)[:S])
    d["offs2"] = striped8(np.stack([np.random.permutation(T2)[:S] for _ in range(8)]))
    d["offs3"] = striped8(np.stack([np.random.permutation(T2)[:P] for _ in range(8)]))
    d["w1"] = (n((K, H)) / K**0.5 / s * u.T).astype(np.float32)
    d["b1"] = (0.5 * n(H) * u[:, 0]).astype(np.float32)
    d["wgs"] = np.repeat(np.random.uniform(0.5, 2.0, (8, S)), 16, axis=0).astype(np.float32)
    d["wgt"] = np.repeat(np.random.uniform(0.5, 2.0, (8, P)), 16, axis=0).astype(np.float32)
    d["wind"] = (0.9 * n((H, P)) * u).astype(np.float32)
    d["w4_words"], d["w4_scales"] = pack_weight(1.8 * n((H, N)) / H**0.5 / u, "e2m1")
    return d

def reference(tab_words, tab_scales, offs, offs2, offs3, w1, b1, wgs, wgt, wind, w4_words, w4_scales):
    v = unpack_weight(tab_words, tab_scales, "e4m3")[:, unstriped(offs)]
    h = (mxq(f64(w1), 0, "e4m3").T @ v) + f64(b1)[:, None]
    page = put_heads(h, f64(wgs), unstriped8(offs2), T2)
    x = heads(page, f64(wgt), unstriped8(offs3))
    z = mxq(np.maximum(x, f64(wind)), 0, "e4m3")
    w4 = unpack_weight(w4_words, w4_scales, "e2m1")
    y = w4.T @ z
    return 1.0 / (1.0 + np.exp(-y))

@@ -1,0 +1,260 @@
+from contextlib import ExitStack
+
+import concourse.mybir as mybir
+
+K, H, N, T, S, M, T2 = 1024, 1024, 512, 4096, 1024, 1024, 2048
+FLOPS = 2 * K * H * S + 2 * H * N * M
+
+F32 = mybir.dt.float32
+BF16 = mybir.dt.bfloat16
+I32 = mybir.dt.int32
+U32 = mybir.dt.uint32
+U16 = mybir.dt.uint16
+U8 = mybir.dt.uint8
+FP8X4 = mybir.dt.float8_e4m3fn_x4
+FP4X4 = mybir.dt.float4_e2m1fn_x4
+MULT = mybir.AluOpType.mult
+MAX = mybir.AluOpType.max
+ACT = mybir.ActivationFunctionType
+
+P = 128
+PACK = 4
+BANK = 512
+CHUNKS = (256, 256, 256, 128, 128)
+WOVEN_ON_SCALAR = 3
+
+
+def weave(nc, dst, src):
+    nc.scalar.copy(
+        dst.rearrange("p (c j i) -> p c i j", j=PACK, i=PACK),
+        src.rearrange("p (i c j) -> p c i j", j=PACK, i=PACK),
+    )
+
+
+def tile_list_cabin_sway_alarm_kernel(
+    tc, tab_words, tab_scales, offs, offs2, offs3, w1, b1, wgs, wgt, wind, w4_words, w4_scales, out
+):
+    nc = tc.nc
+    with ExitStack() as ctx:
+        keep = ctx.enter_context(tc.tile_pool(name="keep", bufs=1))
+        big = ctx.enter_context(tc.tile_pool(name="big", bufs=2))
+        raw = ctx.enter_context(tc.tile_pool(name="raw", bufs=4))
+        woven = ctx.enter_context(tc.tile_pool(name="woven", bufs=2))
+        h_banks = ctx.enter_context(tc.psum_pool(name="h_banks", bufs=4))
+        y_banks = ctx.enter_context(tc.psum_pool(name="y_banks", bufs=4))
+
+        pick = keep.tile([P, S // 16], U16, name="pick")
+        slot = keep.tile([P, S // 16], U16, name="slot")
+        order = keep.tile([P, M // 16], U16, name="order")
+        bias = keep.tile([P, 2, PACK], F32, name="bias")
+        nc.sync.dma_start(pick[:], offs)
+        nc.sync.dma_start(slot[:], offs2)
+        nc.sync.dma_start(order[:], offs3)
+        nc.sync.dma_start(bias[:], b1.rearrange("(b p i) -> p b i", b=2, i=PACK))
+
+        tab_planes = keep.tile([P, T], U8, name="tab_planes", align_bytes=64)
+        nc.vector.memset(tab_planes[:].bitcast(I32), 0)
+        for q in range(4):
+            nc.scalar.dma_start(
+                tab_planes[32 * q : 32 * q + 8, :].bitcast(I32),
+                tab_scales[:, 4 * q : 4 * q + 4, :].bitcast(I32),
+            )
+
+        def load_table(a):
+            words = big.tile([P, T], I32, name="big", align_bytes=64)
+            nc.sync.dma_start(words[:], tab_words[a].rearrange("p t i -> p (t i)").bitcast(I32))
+            return words
+
+        def load_w1(b, a):
+            rows = raw.tile([P, PACK * BANK], F32, name="raw", align_bytes=64)
+            nc.sync.dma_start(
+                rows[:].rearrange("p (j c) -> p j c", j=PACK),
+                w1[BANK * a : BANK * (a + 1), BANK * b : BANK * (b + 1)].rearrange("(p j) c -> p j c", j=PACK),
+            )
+            return rows
+
+        def load_wind(b):
+            rows = big.tile([P, PACK * M], F32, name="big", align_bytes=64)
+            nc.sync.dma_start(rows[:], wind[BANK * b : BANK * (b + 1), :].rearrange("(p i) m -> p (i m)", i=PACK))
+            return rows
+
+        table = [None, None]
+        w1_rows = {}
+        table[0] = load_table(0)
+        w1_rows[0, 0] = load_w1(0, 0)
+        w1_rows[0, 1] = load_w1(0, 1)
+        table[1] = load_table(1)
+        wgs_sb = keep.tile([P, S], F32, name="wgs_sb")
+        nc.sync.dma_start(wgs_sb[:], wgs)
+        w1_rows[1, 0] = load_w1(1, 0)
+        w1_rows[1, 1] = load_w1(1, 1)
+        wgt_sb = keep.tile([P, M], F32, name="wgt_sb")
+        nc.sync.dma_start(wgt_sb[:], wgt)
+
+        pages = [keep.tile([P, T2], F32, name="page%d" % i) for i in range(PACK)]
+        for page in pages:
+            nc.vector.memset(page[:], 0.0)
+        w4_planes = keep.tile([P, 2, N], U8, name="w4_planes", align_bytes=64)
+        nc.vector.memset(w4_planes[:].bitcast(I32), 0)
+
+        v_words = [keep.tile([P, S], U32, name="v_words%d" % a, align_bytes=64) for a in range(2)]
+        v_planes = keep.tile([P, S], U8, name="v_planes", align_bytes=64)
+        w1_words = {}
+        w1_planes = {}
+
+        def quantise_w1(b, a):
+            grouped = woven.tile([P, PACK * BANK], BF16, name="grouped", align_bytes=64)
+            nc.scalar.copy(
+                grouped[:].rearrange("p (i q j) -> p q j i", i=PACK, j=PACK),
+                w1_rows[b, a][:].rearrange("p (j q i) -> p q j i", i=PACK, j=PACK),
+            )
+            w1_words[b, a] = keep.tile([P, BANK], U32, name="w1_words%d%d" % (b, a), align_bytes=64)
+            w1_planes[b, a] = keep.tile([P, BANK], U8, name="w1_planes%d%d" % (b, a), align_bytes=64)
+            nc.vector.quantize_mx(w1_words[b, a][:].bitcast(FP8X4), w1_planes[b, a][:], grouped[:])
+
+        nc.vector.tensor_copy(v_words[0][:], table[0][:].bitcast(U32).indirect(pick[:]))
+        nc.vector.tensor_copy(v_planes[:], tab_planes[:].indirect(pick[:]))
+        quantise_w1(0, 0)
+        quantise_w1(0, 1)
+        for half in range(2):
+            nc.vector.tensor_copy(
+                v_words[1][:, BANK * half : BANK * (half + 1)],
+                table[1][:].bitcast(U32).indirect(pick[:, 32 * half : 32 * (half + 1)]),
+            )
+
+        wind_rows = [load_wind(0), load_wind(1)]
+        w4_sb = keep.tile([P, 2, 2 * N], U8, name="w4_sb", align_bytes=64)
+        nc.sync.dma_start(w4_sb[:].bitcast(I32), w4_words.rearrange("b p n -> p b n").bitcast(I32))
+        for q in range(4):
+            nc.sync.dma_start(
+                w4_planes[32 * q : 32 * q + 4, :, :].bitcast(I32),
+                w4_scales[:, 4 * q : 4 * q + 4, :].rearrange("b q n -> q b n").bitcast(I32),
+            )
+
+        h = [keep.tile([P, S], F32, name="h%d" % t, align_bytes=64) for t in range(2 * PACK)]
+
+        def features(b, i):
+            for half in range(2):
+                cols = slice(BANK * half, BANK * (half + 1))
+                acc = h_banks.tile([P, BANK], F32, name="acc")
+                for a in range(2):
+                    nc.tensor.matmul_mx(
+                        acc[:],
+                        lhsT=w1_words[b, a][:, P * i : P * (i + 1)].bitcast(FP8X4),
+                        lhsT_scale=w1_planes[b, a][:, P * i : P * (i + 1)],
+                        rhs=v_words[a][:, cols].bitcast(FP8X4),
+                        rhs_scale=v_planes[4 * a : P, cols],
+                        start=(a == 0),
+                        stop=(a == 1),
+                    )
+                nc.scalar.activation(h[PACK * b + i][:, cols], acc[:], ACT.Identity, bias=bias[:, b, i : i + 1])
+
+        def hang(b, i, lo, hi):
+            nc.vector.tensor_tensor(
+                pages[i][:].indirect(slot[:, lo // 16 : hi // 16]), h[PACK * b + i][:, lo:hi], wgs_sb[:, lo:hi], MULT
+            )
+
+        def inspect(dst, i, lo, hi):
+            nc.vector.tensor_tensor(dst, pages[i][:].indirect(order[:, lo // 16 : hi // 16]), wgt_sb[:, lo:hi], MULT)
+
+        z_words = [keep.tile([P, M], U32, name="z_words%d" % b, align_bytes=64) for b in range(2)]
+        z_planes = [keep.tile([P, M], U8, name="z_planes%d" % b, align_bytes=64) for b in range(2)]
+        wind_bf = [keep.tile([P, PACK * M], BF16, name="wind_bf%d" % b, align_bytes=64) for b in range(2)]
+
+        def quantise_z(b, lo, hi, z):
+            nc.vector.quantize_mx(z_words[b][:, lo:hi].bitcast(FP8X4), z_planes[b][:, lo:hi], z)
+
+        for i in range(PACK):
+            features(0, i)
+        hang(0, 0, 0, BANK)
+        hang(0, 0, BANK, S)
+        hang(0, 1, 0, S)
+        quantise_w1(1, 0)
+        quantise_w1(1, 1)
+        hang(0, 2, 0, S)
+        hang(0, 3, 0, S)
+        for i in range(PACK):
+            features(1, i)
+        for b in range(2):
+            weave(nc, wind_bf[b][:], wind_rows[b][:])
+        for half in range(2):
+            x = raw.tile([P, PACK * BANK], F32, name="raw", align_bytes=64)
+            for i in range(PACK):
+                inspect(x[:, BANK * i : BANK * (i + 1)], i, BANK * half, BANK * (half + 1))
+            weave(nc, h[half][:].bitcast(BF16), x[:])
+
+        for i in range(PACK):
+            hang(1, i, 0, S)
+            if i in (1, 2):
+                half = i - 1
+                lo, hi = BANK * half, BANK * (half + 1)
+                z = h[PACK + half][:].bitcast(BF16)
+                nc.vector.tensor_tensor(z, h[half][:].bitcast(BF16), wind_bf[0][:, PACK * lo : PACK * hi], MAX)
+                quantise_z(0, lo, hi, z)
+
+        starts = [sum(CHUNKS[:c]) for c in range(len(CHUNKS))]
+        xs = [keep.tile([P, PACK * w], F32, name="x%d" % c, align_bytes=64) for c, w in enumerate(CHUNKS)]
+        out_rows = out.rearrange("(t p) m -> p t m", p=P)
+
+        def x_bf(c):
+            return xs[c + 2][:, PACK * CHUNKS[c + 2] - 2 * CHUNKS[c] :].bitcast(BF16)
+
+        def z_bf(c):
+            return h[c][:, : 2 * CHUNKS[c]].bitcast(BF16)
+
+        def gather_chunk(c, planes):
+            w = CHUNKS[c]
+            for i in planes:
+                inspect(xs[c][:, w * i : w * (i + 1)], i, starts[c], starts[c] + w)
+
+        def floor_chunk(c):
+            lo, hi = starts[c], starts[c] + CHUNKS[c]
+            limit = wind_bf[1][:, PACK * lo : PACK * hi]
+            if c < WOVEN_ON_SCALAR:
+                nc.vector.tensor_tensor(z_bf(c), x_bf(c), limit, MAX)
+            else:
+                nc.vector.tensor_tensor(
+                    z_bf(c).rearrange("p (m i) -> p m i", i=PACK),
+                    xs[c][:].rearrange("p (i m) -> p m i", i=PACK),
+                    limit.rearrange("p (m i) -> p m i", i=PACK),
+                    MAX,
+                )
+
+        def score_chunk(c):
+            lo, w = starts[c], CHUNKS[c]
+            quantise_z(1, lo, lo + w, z_bf(c))
+            scores = keep.tile([P, N // P, w], F32, name="scores%d" % c)
+            for s in range(w // P):
+                cols = slice(lo + P * s, lo + P * (s + 1))
+                y = y_banks.tile([P, N // P, P], F32, name="y")
+                for t in range(N // P):
+                    for b in range(2):
+                        nc.tensor.matmul_mx(
+                            y[:, t, :],
+                            lhsT=w4_sb[:, b, 2 * P * t : 2 * P * (t + 1)].bitcast(FP4X4),
+                            lhsT_scale=w4_planes[:, b, P * t : P * (t + 1)],
+                            rhs=z_words[b][:, cols].bitcast(FP8X4),
+                            rhs_scale=z_planes[b][:, cols],
+                            start=(b == 0),
+                            stop=(b == 1),
+                        )
+                nc.scalar.activation(scores[:, :, P * s : P * (s + 1)], y[:], ACT.Sigmoid)
+            nc.sync.dma_start(out_rows[:, :, lo : lo + w], scores[:])
+
+        for c in range(2):
+            gather_chunk(c, range(PACK))
+            weave(nc, x_bf(c), xs[c][:])
+        gather_chunk(2, (0, 1))
+        floor_chunk(0)
+        gather_chunk(2, (2,))
+        score_chunk(0)
+        gather_chunk(2, (3,))
+        weave(nc, x_bf(2), xs[2][:])
+        for c in (3, 4):
+            floor_chunk(c - 2)
+            gather_chunk(c, (0,))
+            score_chunk(c - 2)
+            gather_chunk(c, (1, 2, 3))
+        for c in (3, 4):
+            floor_chunk(c)
+            score_chunk(c)

@@ -19,13 +19,17 @@ ACT = mybir.ActivationFunctionType
 
 P = 128
 PACK = 4
+PASS = P * PACK
 BANK = 512
+GROUP = 16
+QUADRANT = 32
+FIRST = 256
 CHUNKS = (256, 256, 256, 128, 128)
-WOVEN_ON_SCALAR = 3
+SCALAR_CHUNKS = 3
 
 
-def weave(nc, dst, src):
-    nc.scalar.copy(
+def interleave(copy, dst, src):
+    copy(
         dst.rearrange("p (c j i) -> p c i j", j=PACK, i=PACK),
         src.rearrange("p (i c j) -> p c i j", j=PACK, i=PACK),
     )
@@ -39,25 +43,25 @@ def tile_list_cabin_sway_alarm_kernel(
         keep = ctx.enter_context(tc.tile_pool(name="keep", bufs=1))
         big = ctx.enter_context(tc.tile_pool(name="big", bufs=2))
         raw = ctx.enter_context(tc.tile_pool(name="raw", bufs=4))
-        woven = ctx.enter_context(tc.tile_pool(name="woven", bufs=2))
+        grouped_w1 = ctx.enter_context(tc.tile_pool(name="grouped_w1", bufs=2))
         h_banks = ctx.enter_context(tc.psum_pool(name="h_banks", bufs=4))
         y_banks = ctx.enter_context(tc.psum_pool(name="y_banks", bufs=4))
 
-        pick = keep.tile([P, S // 16], U16, name="pick")
-        slot = keep.tile([P, S // 16], U16, name="slot")
-        order = keep.tile([P, M // 16], U16, name="order")
+        pick = keep.tile([P, S // GROUP], U16, name="pick")
+        slot = keep.tile([P, S // GROUP], U16, name="slot")
+        order = keep.tile([P, M // GROUP], U16, name="order")
         bias = keep.tile([P, 2, PACK], F32, name="bias")
         nc.sync.dma_start(pick[:], offs)
         nc.sync.dma_start(slot[:], offs2)
         nc.sync.dma_start(order[:], offs3)
         nc.sync.dma_start(bias[:], b1.rearrange("(b p i) -> p b i", b=2, i=PACK))
 
-        tab_planes = keep.tile([P, T], U8, name="tab_planes", align_bytes=64)
-        nc.vector.memset(tab_planes[:].bitcast(I32), 0)
-        for q in range(4):
+        tab_scale_rows = keep.tile([P, T], U8, name="tab_scale_rows", align_bytes=64)
+        nc.vector.memset(tab_scale_rows[:].bitcast(I32), 0)
+        for quad in range(P // QUADRANT):
             nc.scalar.dma_start(
-                tab_planes[32 * q : 32 * q + 8, :].bitcast(I32),
-                tab_scales[:, 4 * q : 4 * q + 4, :].bitcast(I32),
+                tab_scale_rows[QUADRANT * quad : QUADRANT * quad + 2 * PACK, :].bitcast(I32),
+                tab_scales[:, PACK * quad : PACK * (quad + 1), :].bitcast(I32),
             )
 
         def load_table(a):
@@ -66,19 +70,19 @@ def tile_list_cabin_sway_alarm_kernel(
             return words
 
         def load_w1(b, a):
-            rows = raw.tile([P, PACK * BANK], F32, name="raw", align_bytes=64)
+            rows = raw.tile([P, PACK * PASS], F32, name="raw", align_bytes=64)
             nc.sync.dma_start(
                 rows[:].rearrange("p (j c) -> p j c", j=PACK),
-                w1[BANK * a : BANK * (a + 1), BANK * b : BANK * (b + 1)].rearrange("(p j) c -> p j c", j=PACK),
+                w1[PASS * a : PASS * (a + 1), PASS * b : PASS * (b + 1)].rearrange("(p j) c -> p j c", j=PACK),
             )
             return rows
 
         def load_wind(b):
             rows = big.tile([P, PACK * M], F32, name="big", align_bytes=64)
-            nc.sync.dma_start(rows[:], wind[BANK * b : BANK * (b + 1), :].rearrange("(p i) m -> p (i m)", i=PACK))
+            nc.sync.dma_start(rows[:], wind[PASS * b : PASS * (b + 1), :].rearrange("(p i) m -> p (i m)", i=PACK))
             return rows
 
-        table = [None, None]
+        table = {}
         w1_rows = {}
         table[0] = load_table(0)
         w1_rows[0, 0] = load_w1(0, 0)
@@ -94,94 +98,103 @@ def tile_list_cabin_sway_alarm_kernel(
         pages = [keep.tile([P, T2], F32, name="page%d" % i) for i in range(PACK)]
         for page in pages:
             nc.vector.memset(page[:], 0.0)
-        w4_planes = keep.tile([P, 2, N], U8, name="w4_planes", align_bytes=64)
-        nc.vector.memset(w4_planes[:].bitcast(I32), 0)
+        w4_scale_rows = keep.tile([P, 2, N], U8, name="w4_scale_rows", align_bytes=64)
+        nc.vector.memset(w4_scale_rows[:].bitcast(I32), 0)
 
         v_words = [keep.tile([P, S], U32, name="v_words%d" % a, align_bytes=64) for a in range(2)]
-        v_planes = keep.tile([P, S], U8, name="v_planes", align_bytes=64)
+        v_scales = keep.tile([P, S], U8, name="v_scales", align_bytes=64)
         w1_words = {}
-        w1_planes = {}
+        w1_scales = {}
 
         def quantise_w1(b, a):
-            grouped = woven.tile([P, PACK * BANK], BF16, name="grouped", align_bytes=64)
+            grouped = grouped_w1.tile([P, PACK * PASS], BF16, name="grouped", align_bytes=64)
             nc.scalar.copy(
                 grouped[:].rearrange("p (i q j) -> p q j i", i=PACK, j=PACK),
                 w1_rows[b, a][:].rearrange("p (j q i) -> p q j i", i=PACK, j=PACK),
             )
-            w1_words[b, a] = keep.tile([P, BANK], U32, name="w1_words%d%d" % (b, a), align_bytes=64)
-            w1_planes[b, a] = keep.tile([P, BANK], U8, name="w1_planes%d%d" % (b, a), align_bytes=64)
-            nc.vector.quantize_mx(w1_words[b, a][:].bitcast(FP8X4), w1_planes[b, a][:], grouped[:])
+            w1_words[b, a] = keep.tile([P, PASS], U32, name="w1_words%d%d" % (b, a), align_bytes=64)
+            w1_scales[b, a] = keep.tile([P, PASS], U8, name="w1_scales%d%d" % (b, a), align_bytes=64)
+            nc.vector.quantize_mx(w1_words[b, a][:].bitcast(FP8X4), w1_scales[b, a][:], grouped[:])
 
         nc.vector.tensor_copy(v_words[0][:], table[0][:].bitcast(U32).indirect(pick[:]))
-        nc.vector.tensor_copy(v_planes[:], tab_planes[:].indirect(pick[:]))
+        nc.vector.tensor_copy(v_scales[:], tab_scale_rows[:].indirect(pick[:]))
         quantise_w1(0, 0)
         quantise_w1(0, 1)
-        for half in range(2):
+        for lo in (0, BANK):
             nc.vector.tensor_copy(
-                v_words[1][:, BANK * half : BANK * (half + 1)],
-                table[1][:].bitcast(U32).indirect(pick[:, 32 * half : 32 * (half + 1)]),
+                v_words[1][:, lo : lo + BANK],
+                table[1][:].bitcast(U32).indirect(pick[:, lo // GROUP : (lo + BANK) // GROUP]),
             )
 
         wind_rows = [load_wind(0), load_wind(1)]
         w4_sb = keep.tile([P, 2, 2 * N], U8, name="w4_sb", align_bytes=64)
         nc.sync.dma_start(w4_sb[:].bitcast(I32), w4_words.rearrange("b p n -> p b n").bitcast(I32))
-        for q in range(4):
+        for quad in range(P // QUADRANT):
             nc.sync.dma_start(
-                w4_planes[32 * q : 32 * q + 4, :, :].bitcast(I32),
-                w4_scales[:, 4 * q : 4 * q + 4, :].rearrange("b q n -> q b n").bitcast(I32),
+                w4_scale_rows[QUADRANT * quad : QUADRANT * quad + PACK, :, :].bitcast(I32),
+                w4_scales[:, PACK * quad : PACK * (quad + 1), :].rearrange("b q n -> q b n").bitcast(I32),
             )
 
         h = [keep.tile([P, S], F32, name="h%d" % t, align_bytes=64) for t in range(2 * PACK)]
 
-        def features(b, i):
-            for half in range(2):
-                cols = slice(BANK * half, BANK * (half + 1))
+        def features(b, i, cuts):
+            for lo, hi in zip(cuts, cuts[1:]):
                 acc = h_banks.tile([P, BANK], F32, name="acc")
                 for a in range(2):
                     nc.tensor.matmul_mx(
-                        acc[:],
+                        acc[:, : hi - lo],
                         lhsT=w1_words[b, a][:, P * i : P * (i + 1)].bitcast(FP8X4),
-                        lhsT_scale=w1_planes[b, a][:, P * i : P * (i + 1)],
-                        rhs=v_words[a][:, cols].bitcast(FP8X4),
-                        rhs_scale=v_planes[4 * a : P, cols],
+                        lhsT_scale=w1_scales[b, a][:, P * i : P * (i + 1)],
+                        rhs=v_words[a][:, lo:hi].bitcast(FP8X4),
+                        rhs_scale=v_scales[PACK * a : P, lo:hi],
                         start=(a == 0),
                         stop=(a == 1),
                     )
-                nc.scalar.activation(h[PACK * b + i][:, cols], acc[:], ACT.Identity, bias=bias[:, b, i : i + 1])
+                nc.scalar.activation(
+                    h[PACK * b + i][:, lo:hi], acc[:, : hi - lo], ACT.Identity, bias=bias[:, b, i : i + 1]
+                )
 
         def hang(b, i, lo, hi):
             nc.vector.tensor_tensor(
-                pages[i][:].indirect(slot[:, lo // 16 : hi // 16]), h[PACK * b + i][:, lo:hi], wgs_sb[:, lo:hi], MULT
+                pages[i][:].indirect(slot[:, lo // GROUP : hi // GROUP]),
+                h[PACK * b + i][:, lo:hi],
+                wgs_sb[:, lo:hi],
+                MULT,
             )
 
         def inspect(dst, i, lo, hi):
-            nc.vector.tensor_tensor(dst, pages[i][:].indirect(order[:, lo // 16 : hi // 16]), wgt_sb[:, lo:hi], MULT)
+            nc.vector.tensor_tensor(
+                dst, pages[i][:].indirect(order[:, lo // GROUP : hi // GROUP]), wgt_sb[:, lo:hi], MULT
+            )
 
         z_words = [keep.tile([P, M], U32, name="z_words%d" % b, align_bytes=64) for b in range(2)]
-        z_planes = [keep.tile([P, M], U8, name="z_planes%d" % b, align_bytes=64) for b in range(2)]
+        z_scales = [keep.tile([P, M], U8, name="z_scales%d" % b, align_bytes=64) for b in range(2)]
         wind_bf = [keep.tile([P, PACK * M], BF16, name="wind_bf%d" % b, align_bytes=64) for b in range(2)]
 
         def quantise_z(b, lo, hi, z):
-            nc.vector.quantize_mx(z_words[b][:, lo:hi].bitcast(FP8X4), z_planes[b][:, lo:hi], z)
+            nc.vector.quantize_mx(z_words[b][:, lo:hi].bitcast(FP8X4), z_scales[b][:, lo:hi], z)
 
-        for i in range(PACK):
-            features(0, i)
-        hang(0, 0, 0, BANK)
-        hang(0, 0, BANK, S)
+        features(0, 0, (0, FIRST, BANK, S))
+        for i in range(1, PACK):
+            features(0, i, (0, BANK, S))
+        hang(0, 0, 0, FIRST)
+        hang(0, 0, FIRST, S)
         hang(0, 1, 0, S)
         quantise_w1(1, 0)
         quantise_w1(1, 1)
         hang(0, 2, 0, S)
         hang(0, 3, 0, S)
         for i in range(PACK):
-            features(1, i)
+            features(1, i, (0, BANK, S))
+        warm = keep.tile([P, 1], F32, name="warm")
+        nc.scalar.activation(warm[:], h[2 * PACK - 1][:, 0:1], ACT.Sigmoid)
         for b in range(2):
-            weave(nc, wind_bf[b][:], wind_rows[b][:])
+            interleave(nc.scalar.copy, wind_bf[b][:], wind_rows[b][:])
         for half in range(2):
             x = raw.tile([P, PACK * BANK], F32, name="raw", align_bytes=64)
             for i in range(PACK):
                 inspect(x[:, BANK * i : BANK * (i + 1)], i, BANK * half, BANK * (half + 1))
-            weave(nc, h[half][:].bitcast(BF16), x[:])
+            interleave(nc.scalar.copy, h[half][:].bitcast(BF16), x[:])
 
         for i in range(PACK):
             hang(1, i, 0, S)
@@ -197,7 +210,10 @@ def tile_list_cabin_sway_alarm_kernel(
         out_rows = out.rearrange("(t p) m -> p t m", p=P)
 
         def x_bf(c):
-            return xs[c + 2][:, PACK * CHUNKS[c + 2] - 2 * CHUNKS[c] :].bitcast(BF16)
+            room = 2 * CHUNKS[c]
+            if c < SCALAR_CHUNKS:
+                return xs[c + 2][:, PACK * CHUNKS[c + 2] - room :].bitcast(BF16)
+            return h[2 * PACK - 2][:, room * (c - SCALAR_CHUNKS) : room * (c - SCALAR_CHUNKS + 1)].bitcast(BF16)
 
         def z_bf(c):
             return h[c][:, : 2 * CHUNKS[c]].bitcast(BF16)
@@ -209,16 +225,7 @@ def tile_list_cabin_sway_alarm_kernel(
 
         def floor_chunk(c):
             lo, hi = starts[c], starts[c] + CHUNKS[c]
-            limit = wind_bf[1][:, PACK * lo : PACK * hi]
-            if c < WOVEN_ON_SCALAR:
-                nc.vector.tensor_tensor(z_bf(c), x_bf(c), limit, MAX)
-            else:
-                nc.vector.tensor_tensor(
-                    z_bf(c).rearrange("p (m i) -> p m i", i=PACK),
-                    xs[c][:].rearrange("p (i m) -> p m i", i=PACK),
-                    limit.rearrange("p (m i) -> p m i", i=PACK),
-                    MAX,
-                )
+            nc.vector.tensor_tensor(z_bf(c), x_bf(c), wind_bf[1][:, PACK * lo : PACK * hi], MAX)
 
         def score_chunk(c):
             lo, w = starts[c], CHUNKS[c]
@@ -226,35 +233,38 @@ def tile_list_cabin_sway_alarm_kernel(
             scores = keep.tile([P, N // P, w], F32, name="scores%d" % c)
             for s in range(w // P):
                 cols = slice(lo + P * s, lo + P * (s + 1))
-                y = y_banks.tile([P, N // P, P], F32, name="y")
-                for t in range(N // P):
-                    for b in range(2):
+                y = y_banks.tile([P, BANK], F32, name="y")
+                for b in range(2):
+                    for t in range(N // P):
                         nc.tensor.matmul_mx(
-                            y[:, t, :],
+                            y[:, P * t : P * (t + 1)],
                             lhsT=w4_sb[:, b, 2 * P * t : 2 * P * (t + 1)].bitcast(FP4X4),
-                            lhsT_scale=w4_planes[:, b, P * t : P * (t + 1)],
+                            lhsT_scale=w4_scale_rows[:, b, P * t : P * (t + 1)],
                             rhs=z_words[b][:, cols].bitcast(FP8X4),
-                            rhs_scale=z_planes[b][:, cols],
-                            start=(b == 0),
-                            stop=(b == 1),
+                            rhs_scale=z_scales[b][:, cols],
+                            start=(b == 0 and t == 0),
+                            stop=(b == 1 and t == N // P - 1),
                         )
-                nc.scalar.activation(scores[:, :, P * s : P * (s + 1)], y[:], ACT.Sigmoid)
+                nc.scalar.activation(
+                    scores[:, :, P * s : P * (s + 1)], y[:].rearrange("p (t m) -> p t m", m=P), ACT.Sigmoid
+                )
             nc.sync.dma_start(out_rows[:, :, lo : lo + w], scores[:])
 
         for c in range(2):
             gather_chunk(c, range(PACK))
-            weave(nc, x_bf(c), xs[c][:])
+            interleave(nc.scalar.copy, x_bf(c), xs[c][:])
         gather_chunk(2, (0, 1))
         floor_chunk(0)
         gather_chunk(2, (2,))
         score_chunk(0)
         gather_chunk(2, (3,))
-        weave(nc, x_bf(2), xs[2][:])
-        for c in (3, 4):
+        interleave(nc.scalar.copy, x_bf(2), xs[2][:])
+        for c in range(SCALAR_CHUNKS, len(CHUNKS)):
             floor_chunk(c - 2)
             gather_chunk(c, (0,))
             score_chunk(c - 2)
-            gather_chunk(c, (1, 2, 3))
-        for c in (3, 4):
+            gather_chunk(c, range(1, PACK))
+            interleave(nc.vector.tensor_copy, x_bf(c), xs[c][:])
+        for c in range(SCALAR_CHUNKS, len(CHUNKS)):
             floor_chunk(c)
             score_chunk(c)

from contextlib import ExitStack

import concourse.mybir as mybir

K, H, N, T, S, M, T2 = 1024, 1024, 512, 4096, 1024, 1024, 2048
FLOPS = 2 * K * H * S + 2 * H * N * M

F32 = mybir.dt.float32
BF16 = mybir.dt.bfloat16
I32 = mybir.dt.int32
U32 = mybir.dt.uint32
U16 = mybir.dt.uint16
U8 = mybir.dt.uint8
FP8X4 = mybir.dt.float8_e4m3fn_x4
FP4X4 = mybir.dt.float4_e2m1fn_x4
MULT = mybir.AluOpType.mult
MAX = mybir.AluOpType.max
ACT = mybir.ActivationFunctionType

P = 128
PACK = 4
PASS = P * PACK
BANK = 512
GROUP = 16
QUADRANT = 32
FIRST = 256
CHUNKS = (256, 256, 256, 128, 128)
SCALAR_CHUNKS = 3


def interleave(copy, dst, src):
    copy(
        dst.rearrange("p (c j i) -> p c i j", j=PACK, i=PACK),
        src.rearrange("p (i c j) -> p c i j", j=PACK, i=PACK),
    )


def tile_list_cabin_sway_alarm_kernel(
    tc, tab_words, tab_scales, offs, offs2, offs3, w1, b1, wgs, wgt, wind, w4_words, w4_scales, out
):
    nc = tc.nc
    with ExitStack() as ctx:
        keep = ctx.enter_context(tc.tile_pool(name="keep", bufs=1))
        big = ctx.enter_context(tc.tile_pool(name="big", bufs=2))
        raw = ctx.enter_context(tc.tile_pool(name="raw", bufs=4))
        grouped_w1 = ctx.enter_context(tc.tile_pool(name="grouped_w1", bufs=2))
        h_banks = ctx.enter_context(tc.psum_pool(name="h_banks", bufs=4))
        y_banks = ctx.enter_context(tc.psum_pool(name="y_banks", bufs=4))

        pick = keep.tile([P, S // GROUP], U16, name="pick")
        slot = keep.tile([P, S // GROUP], U16, name="slot")
        order = keep.tile([P, M // GROUP], U16, name="order")
        bias = keep.tile([P, 2, PACK], F32, name="bias")
        nc.sync.dma_start(pick[:], offs)
        nc.sync.dma_start(slot[:], offs2)
        nc.sync.dma_start(order[:], offs3)
        nc.sync.dma_start(bias[:], b1.rearrange("(b p i) -> p b i", b=2, i=PACK))

        tab_scale_rows = keep.tile([P, T], U8, name="tab_scale_rows", align_bytes=64)
        nc.vector.memset(tab_scale_rows[:].bitcast(I32), 0)
        for quad in range(P // QUADRANT):
            nc.scalar.dma_start(
                tab_scale_rows[QUADRANT * quad : QUADRANT * quad + 2 * PACK, :].bitcast(I32),
                tab_scales[:, PACK * quad : PACK * (quad + 1), :].bitcast(I32),
            )

        def load_table(a):
            words = big.tile([P, T], I32, name="big", align_bytes=64)
            nc.sync.dma_start(words[:], tab_words[a].rearrange("p t i -> p (t i)").bitcast(I32))
            return words

        def load_w1(b, a):
            rows = raw.tile([P, PACK * PASS], F32, name="raw", align_bytes=64)
            nc.sync.dma_start(
                rows[:].rearrange("p (j c) -> p j c", j=PACK),
                w1[PASS * a : PASS * (a + 1), PASS * b : PASS * (b + 1)].rearrange("(p j) c -> p j c", j=PACK),
            )
            return rows

        def load_wind(b):
            rows = big.tile([P, PACK * M], F32, name="big", align_bytes=64)
            nc.sync.dma_start(rows[:], wind[PASS * b : PASS * (b + 1), :].rearrange("(p i) m -> p (i m)", i=PACK))
            return rows

        table = {}
        w1_rows = {}
        table[0] = load_table(0)
        w1_rows[0, 0] = load_w1(0, 0)
        w1_rows[0, 1] = load_w1(0, 1)
        table[1] = load_table(1)
        wgs_sb = keep.tile([P, S], F32, name="wgs_sb")
        nc.sync.dma_start(wgs_sb[:], wgs)
        w1_rows[1, 0] = load_w1(1, 0)
        w1_rows[1, 1] = load_w1(1, 1)
        wgt_sb = keep.tile([P, M], F32, name="wgt_sb")
        nc.sync.dma_start(wgt_sb[:], wgt)

        pages = [keep.tile([P, T2], F32, name="page%d" % i) for i in range(PACK)]
        for page in pages:
            nc.vector.memset(page[:], 0.0)
        w4_scale_rows = keep.tile([P, 2, N], U8, name="w4_scale_rows", align_bytes=64)
        nc.vector.memset(w4_scale_rows[:].bitcast(I32), 0)

        v_words = [keep.tile([P, S], U32, name="v_words%d" % a, align_bytes=64) for a in range(2)]
        v_scales = keep.tile([P, S], U8, name="v_scales", align_bytes=64)
        w1_words = {}
        w1_scales = {}

        def quantise_w1(b, a):
            grouped = grouped_w1.tile([P, PACK * PASS], BF16, name="grouped", align_bytes=64)
            nc.scalar.copy(
                grouped[:].rearrange("p (i q j) -> p q j i", i=PACK, j=PACK),
                w1_rows[b, a][:].rearrange("p (j q i) -> p q j i", i=PACK, j=PACK),
            )
            w1_words[b, a] = keep.tile([P, PASS], U32, name="w1_words%d%d" % (b, a), align_bytes=64)
            w1_scales[b, a] = keep.tile([P, PASS], U8, name="w1_scales%d%d" % (b, a), align_bytes=64)
            nc.vector.quantize_mx(w1_words[b, a][:].bitcast(FP8X4), w1_scales[b, a][:], grouped[:])

        nc.vector.tensor_copy(v_words[0][:], table[0][:].bitcast(U32).indirect(pick[:]))
        nc.vector.tensor_copy(v_scales[:], tab_scale_rows[:].indirect(pick[:]))
        quantise_w1(0, 0)
        quantise_w1(0, 1)
        for lo in (0, BANK):
            nc.vector.tensor_copy(
                v_words[1][:, lo : lo + BANK],
                table[1][:].bitcast(U32).indirect(pick[:, lo // GROUP : (lo + BANK) // GROUP]),
            )

        wind_rows = [load_wind(0), load_wind(1)]
        w4_sb = keep.tile([P, 2, 2 * N], U8, name="w4_sb", align_bytes=64)
        nc.sync.dma_start(w4_sb[:].bitcast(I32), w4_words.rearrange("b p n -> p b n").bitcast(I32))
        for quad in range(P // QUADRANT):
            nc.sync.dma_start(
                w4_scale_rows[QUADRANT * quad : QUADRANT * quad + PACK, :, :].bitcast(I32),
                w4_scales[:, PACK * quad : PACK * (quad + 1), :].rearrange("b q n -> q b n").bitcast(I32),
            )

        h = [keep.tile([P, S], F32, name="h%d" % t, align_bytes=64) for t in range(2 * PACK)]

        def features(b, i, cuts):
            for lo, hi in zip(cuts, cuts[1:]):
                acc = h_banks.tile([P, BANK], F32, name="acc")
                for a in range(2):
                    nc.tensor.matmul_mx(
                        acc[:, : hi - lo],
                        lhsT=w1_words[b, a][:, P * i : P * (i + 1)].bitcast(FP8X4),
                        lhsT_scale=w1_scales[b, a][:, P * i : P * (i + 1)],
                        rhs=v_words[a][:, lo:hi].bitcast(FP8X4),
                        rhs_scale=v_scales[PACK * a : P, lo:hi],
                        start=(a == 0),
                        stop=(a == 1),
                    )
                nc.scalar.activation(
                    h[PACK * b + i][:, lo:hi], acc[:, : hi - lo], ACT.Identity, bias=bias[:, b, i : i + 1]
                )

        def hang(b, i, lo, hi):
            nc.vector.tensor_tensor(
                pages[i][:].indirect(slot[:, lo // GROUP : hi // GROUP]),
                h[PACK * b + i][:, lo:hi],
                wgs_sb[:, lo:hi],
                MULT,
            )

        def inspect(dst, i, lo, hi):
            nc.vector.tensor_tensor(
                dst, pages[i][:].indirect(order[:, lo // GROUP : hi // GROUP]), wgt_sb[:, lo:hi], MULT
            )

        z_words = [keep.tile([P, M], U32, name="z_words%d" % b, align_bytes=64) for b in range(2)]
        z_scales = [keep.tile([P, M], U8, name="z_scales%d" % b, align_bytes=64) for b in range(2)]
        wind_bf = [keep.tile([P, PACK * M], BF16, name="wind_bf%d" % b, align_bytes=64) for b in range(2)]

        def quantise_z(b, lo, hi, z):
            nc.vector.quantize_mx(z_words[b][:, lo:hi].bitcast(FP8X4), z_scales[b][:, lo:hi], z)

        features(0, 0, (0, FIRST, BANK, S))
        for i in range(1, PACK):
            features(0, i, (0, BANK, S))
        hang(0, 0, 0, FIRST)
        hang(0, 0, FIRST, S)
        hang(0, 1, 0, S)
        quantise_w1(1, 0)
        quantise_w1(1, 1)
        hang(0, 2, 0, S)
        hang(0, 3, 0, S)
        for i in range(PACK):
            features(1, i, (0, BANK, S))
        warm = keep.tile([P, 1], F32, name="warm")
        nc.scalar.activation(warm[:], h[2 * PACK - 1][:, 0:1], ACT.Sigmoid)
        for b in range(2):
            interleave(nc.scalar.copy, wind_bf[b][:], wind_rows[b][:])
        for half in range(2):
            x = raw.tile([P, PACK * BANK], F32, name="raw", align_bytes=64)
            for i in range(PACK):
                inspect(x[:, BANK * i : BANK * (i + 1)], i, BANK * half, BANK * (half + 1))
            interleave(nc.scalar.copy, h[half][:].bitcast(BF16), x[:])

        for i in range(PACK):
            hang(1, i, 0, S)
            if i in (1, 2):
                half = i - 1
                lo, hi = BANK * half, BANK * (half + 1)
                z = h[PACK + half][:].bitcast(BF16)
                nc.vector.tensor_tensor(z, h[half][:].bitcast(BF16), wind_bf[0][:, PACK * lo : PACK * hi], MAX)
                quantise_z(0, lo, hi, z)

        starts = [sum(CHUNKS[:c]) for c in range(len(CHUNKS))]
        xs = [keep.tile([P, PACK * w], F32, name="x%d" % c, align_bytes=64) for c, w in enumerate(CHUNKS)]
        out_rows = out.rearrange("(t p) m -> p t m", p=P)

        def x_bf(c):
            room = 2 * CHUNKS[c]
            if c < SCALAR_CHUNKS:
                return xs[c + 2][:, PACK * CHUNKS[c + 2] - room :].bitcast(BF16)
            return h[2 * PACK - 2][:, room * (c - SCALAR_CHUNKS) : room * (c - SCALAR_CHUNKS + 1)].bitcast(BF16)

        def z_bf(c):
            return h[c][:, : 2 * CHUNKS[c]].bitcast(BF16)

        def gather_chunk(c, planes):
            w = CHUNKS[c]
            for i in planes:
                inspect(xs[c][:, w * i : w * (i + 1)], i, starts[c], starts[c] + w)

        def floor_chunk(c):
            lo, hi = starts[c], starts[c] + CHUNKS[c]
            nc.vector.tensor_tensor(z_bf(c), x_bf(c), wind_bf[1][:, PACK * lo : PACK * hi], MAX)

        def score_chunk(c):
            lo, w = starts[c], CHUNKS[c]
            quantise_z(1, lo, lo + w, z_bf(c))
            scores = keep.tile([P, N // P, w], F32, name="scores%d" % c)
            for s in range(w // P):
                cols = slice(lo + P * s, lo + P * (s + 1))
                y = y_banks.tile([P, BANK], F32, name="y")
                for b in range(2):
                    for t in range(N // P):
                        nc.tensor.matmul_mx(
                            y[:, P * t : P * (t + 1)],
                            lhsT=w4_sb[:, b, 2 * P * t : 2 * P * (t + 1)].bitcast(FP4X4),
                            lhsT_scale=w4_scale_rows[:, b, P * t : P * (t + 1)],
                            rhs=z_words[b][:, cols].bitcast(FP8X4),
                            rhs_scale=z_scales[b][:, cols],
                            start=(b == 0 and t == 0),
                            stop=(b == 1 and t == N // P - 1),
                        )
                nc.scalar.activation(
                    scores[:, :, P * s : P * (s + 1)], y[:].rearrange("p (t m) -> p t m", m=P), ACT.Sigmoid
                )
            nc.sync.dma_start(out_rows[:, :, lo : lo + w], scores[:])

        for c in range(2):
            gather_chunk(c, range(PACK))
            interleave(nc.scalar.copy, x_bf(c), xs[c][:])
        gather_chunk(2, (0, 1))
        floor_chunk(0)
        gather_chunk(2, (2,))
        score_chunk(0)
        gather_chunk(2, (3,))
        interleave(nc.scalar.copy, x_bf(2), xs[2][:])
        for c in range(SCALAR_CHUNKS, len(CHUNKS)):
            floor_chunk(c - 2)
            gather_chunk(c, (0,))
            score_chunk(c - 2)
            gather_chunk(c, range(1, PACK))
            interleave(nc.vector.tensor_copy, x_bf(c), xs[c][:])
        for c in range(SCALAR_CHUNKS, len(CHUNKS)):
            floor_chunk(c)
            score_chunk(c)
